import numpy as np
import ml_dtypes


def mxq(x, axis, fmt="e4m3"):
    dtype, down = {"e4m3": (ml_dtypes.float8_e4m3fn, 7), "e5m2": (ml_dtypes.float8_e5m2, 14)}[fmt]
    v = np.moveaxis(np.asarray(x, np.float32).astype(ml_dtypes.bfloat16).astype(np.float64), axis, -1)
    blocks = v.reshape(v.shape[:-1] + (-1, 32))
    amax = np.abs(blocks).max(-1, keepdims=True)
    byte = np.maximum(np.where(amax > 0, np.frexp(amax)[1] - 1 + 127, 0) - down, 1)
    scale = np.exp2(byte - 127.0)
    codes = (blocks / scale).astype(np.float32).astype(dtype).astype(np.float64)
    return np.moveaxis((codes * scale).reshape(v.shape), -1, axis)


WIDE = False


def mx_kscale(k):
    if not WIDE:
        return np.ones(k)
    levels = np.array([10, -10, 5, -5, 0])
    if k % 512:
        return np.exp2(np.random.permutation(np.resize(levels, k // 32))).repeat(32)
    a = np.empty((k // 512, 16))
    for p in range(k // 512):
        a[p, :8] = np.random.permutation(np.resize(levels, 8))
        for g in range(8):
            far = levels[np.abs(levels - a[p, g]) >= 10]
            a[p, g + 8] = far[np.random.randint(len(far))]
    return np.exp2(a.ravel()).repeat(32)


def f64(x):
    return np.asarray(x).astype(np.float64)


def striped(idx):
    return np.tile(idx.reshape(-1, 16).T, (8, 1)).astype(np.uint16)


def unstriped(offs):
    return offs[:16].T.reshape(-1).astype(np.int64)


def striped8(idx):
    return np.concatenate([x.reshape(-1, 16).T for x in idx]).astype(np.uint16)


def runs(offs, k):
    lists = np.stack([offs[16 * r : 16 * r + 16].T.reshape(-1) for r in range(8)]).astype(np.int64)
    return lists[np.arange(k) % 512 // 64]


def pack_weight(w):
    k, n = w.shape
    w = f64(np.asarray(w, np.float32).astype(ml_dtypes.bfloat16)).reshape(k // 32, 32, n)
    amax = np.abs(w).max(1)
    byte = np.clip(np.where(amax > 0, np.frexp(amax)[1] - 1 + 127 - 7, 1), 1, 254)
    scaled = (w * np.exp2(127.0 - byte)[:, None, :]).reshape(k, n).astype(np.float32)
    words = np.ascontiguousarray(scaled.reshape(k // 512, 128, 4, n).transpose(0, 1, 3, 2)).astype(ml_dtypes.float8_e4m3fn).view(np.uint8)
    return words, np.ascontiguousarray(byte.astype(np.uint8).reshape(k // 512, 16, n))


def unpack_weight(words, scales):
    g, p, n, _ = words.shape
    vals = np.ascontiguousarray(words).view(ml_dtypes.float8_e4m3fn).astype(np.float64) * np.repeat(np.exp2(scales.astype(np.float64) - 127.0), 8, axis=1)[..., None]
    return vals.transpose(0, 1, 3, 2).reshape(g * 512, n)


E2M1 = np.array([0.0, 0.5, 1.0, 1.5, 2.0, 3.0, 4.0, 6.0, -0.0, -0.5, -1.0, -1.5, -2.0, -3.0, -4.0, -6.0])


def pack_fp4(w):
    k, n = w.shape
    w = f64(np.asarray(w, np.float32).astype(ml_dtypes.bfloat16)).reshape(k // 32, 32, n)
    amax = np.abs(w).max(1)
    mant, ex = np.frexp(amax / 6.0)
    byte = np.clip(np.where(amax > 0, np.where(mant > 0.5, ex, ex - 1) + 127, 1), 1, 254)
    scaled = (w * np.exp2(127.0 - byte)[:, None, :]).reshape(k, n).astype(np.float32)
    c = np.ascontiguousarray(scaled.reshape(k // 512, 128, 4, n).transpose(0, 1, 3, 2)).astype(ml_dtypes.float4_e2m1fn).view(np.uint8) & 0xF
    words = (c[..., 0::2] | (c[..., 1::2] << 4)).reshape(k // 512, 128, 2 * n)
    return np.ascontiguousarray(words), np.ascontiguousarray(byte.astype(np.uint8).reshape(k // 512, 16, n))


def unpack_fp4(words, scales):
    g, _, n = scales.shape
    words = np.ascontiguousarray(words).reshape(g, 128, n, 2)
    nib = np.empty((g, 128, n, 4), np.uint8)
    nib[..., 0::2] = words & 0xF
    nib[..., 1::2] = words >> 4
    vals = E2M1[nib] * np.repeat(np.exp2(scales.astype(np.float64) - 127.0), 8, axis=1)[..., None]
    return vals.transpose(0, 1, 3, 2).reshape(g * 512, n)


def planes(y):
    n, m = y.shape
    v = y.astype(np.float32).astype(ml_dtypes.bfloat16).astype(np.float64).reshape(n // 32, 32, m)
    top = np.abs(v).max(1)
    byte = np.clip(np.where(top > 0, np.frexp(top)[1] - 1 + 127 - 7, 1), 1, 254)
    codes = (v * np.exp2(127.0 - byte)[:, None, :]).reshape(n, m).astype(np.float32).astype(ml_dtypes.float8_e4m3fn).view(np.uint8)
    words = codes.reshape(n // 512, 128, 4, m).transpose(0, 1, 3, 2)
    return np.ascontiguousarray(words), np.ascontiguousarray(byte.astype(np.uint8).reshape(n // 512, 16, m))


K, T, S, V, N, H, U = 512, 2048, 1024, 512, 512, 512, 1024


def setup_inputs():
    n = np.random.standard_normal
    s = mx_kscale(K)[:, None]
    u = mx_kscale(H)
    packed_xT = pack_weight(n((K, T)) * s)
    packed_w3 = pack_fp4(n((H, N)) / np.sqrt(H) / u[:, None])
    return {
        "x_words": packed_xT[0],
        "x_scales": packed_xT[1],
        "w1": (n((K, H)) / np.sqrt(K) / s * u).astype(np.float32),
        "w2": (n((H, H)) / np.sqrt(H) / u[:, None] * u).astype(np.float32),
        "mem": (n((H, U)) * u[:, None]).astype(np.float32),
        "w3_words": packed_w3[0],
        "w3_scales": packed_w3[1],
        "res": n((N, U)).astype(np.float32),
        "offs": striped(np.random.permutation(T)[:S]),
        "n1": striped8(np.stack([np.random.permutation(S) for _ in range(8)])),
        "n2": striped8(np.stack([np.random.permutation(U)[:V] for _ in range(8)])),
    }


def reference(x_words, x_scales, w1, w2, mem, w3_words, w3_scales, res, offs, n1, n2):
    xq = unpack_weight(x_words, x_scales)[:, unstriped(offs)]
    y = mxq(f64(w1), 0, "e4m3").T @ xq
    ln = y[np.arange(H)[:, None], runs(n1, H)]
    mx = ln.reshape(H, V, 2).max(axis=2)
    mn = ln.reshape(H, V, 2).min(axis=2)
    z = mx - (0.5 * mn)
    h = mxq(f64(w2), 0, "e4m3").T @ mxq(z, 0, "e4m3")
    z2 = f64(mem).copy()
    z2[np.arange(H)[:, None], runs(n2, H)] = h
    out_0 = f64(res) + (unpack_fp4(w3_words, w3_scales).T @ mxq(z2, 0, "e4m3"))
    return (out_0,) + planes(out_0)

@@ -1,0 +1,338 @@
+from contextlib import ExitStack
+
+import concourse.mybir as mybir
+from concourse.masks import make_identity
+
+K, T, S, V, N, H, U = 512, 2048, 1024, 512, 512, 512, 1024
+FLOPS = 2 * K * H * S + 2 * H * H * V + 2 * H * N * U
+
+F32 = mybir.dt.float32
+BF16 = mybir.dt.bfloat16
+I32 = mybir.dt.int32
+U32 = mybir.dt.uint32
+U16 = mybir.dt.uint16
+U8 = mybir.dt.uint8
+FP8X4 = mybir.dt.float8_e4m3fn_x4
+FP4X4 = mybir.dt.float4_e2m1fn_x4
+ALU = mybir.AluOpType
+ACT = mybir.ActivationFunctionType
+
+P = 128
+PACK = 4
+BANK = 512
+VH = V // 2
+W1_PIECES = ((0, 256), (256, 384), (384, 512))
+CHUNKS = (128, 256, 256, 256, 128)
+
+
+def tile_picked_deeppgappage_none_po_kernel(
+    tc, x_words, x_scales, w1, w2, mem, w3_words, w3_scales, res, offs, n1, n2, out_0, out_1, out_2
+):
+    nc = tc.nc
+    with ExitStack() as ctx:
+        lists = ctx.enter_context(tc.tile_pool(name="lists", bufs=1))
+        keep = ctx.enter_context(tc.tile_pool(name="keep", bufs=1))
+        psum = ctx.enter_context(tc.psum_pool(name="psum", bufs=1))
+
+        def sb(shape, dtype, name, tag=None):
+            return keep.tile(shape, dtype, name=name, tag=tag or name, align_bytes=64)
+
+        def bank(number, shape):
+            return psum.tile(shape, F32, name="bank%d" % number)
+
+        def load_scale_rows(queues, plane, rows):
+            for q in range(4):
+                queues[q % 2].dma_start(out=plane[32 * q : 32 * q + 4, :].bitcast(I32), in_=rows[0, 4 * q : 4 * q + 4, :].bitcast(I32))
+
+        def round_and_deal(grouped, raw, m0, copy=nc.scalar.copy):
+            width = raw.shape[2] // PACK
+            copy(
+                out=grouped[:, :, m0 : m0 + width, :].rearrange("p t m j -> p m t j"),
+                in_=raw.rearrange("p j (m t) -> p m t j", t=PACK),
+            )
+
+        def clock(ap, name):
+            tick = sb([P, 1], ap.dtype, name)
+            nc.gpsimd.tensor_copy(out=tick[:], in_=ap)
+
+        offs_t = lists.tile([P, S // 16], U16, name="offs_t")
+        n1_t = lists.tile([P, S // 16], U16, name="n1_t")
+        n2_t = lists.tile([P, V // 16], U16, name="n2_t")
+
+        xs = sb([P, T], U8, "xs")
+        nc.vector.memset(xs[:].bitcast(I32), 0)
+        ident = sb([P, P], F32, "ident")
+        make_identity(nc, ident[:])
+
+        nc.sync.dma_start(offs_t[:], offs)
+        load_scale_rows((nc.sync, nc.scalar), xs, x_scales)
+        xw = sb([P, T], I32, "xw")
+        nc.sync.dma_start(out=xw[:], in_=x_words[0].rearrange("p n t -> p (n t)").bitcast(I32))
+        w1_rows = w1.rearrange("(p j) c -> p j c", j=PACK)
+        w1_raw = []
+        for first, last in W1_PIECES:
+            raw = sb([P, PACK, last - first], F32, "w1_raw%d" % first)
+            nc.sync.dma_start(out=raw[:], in_=w1_rows[:, :, first:last])
+            w1_raw.append(raw)
+        nc.sync.dma_start(n1_t[:], n1)
+        w2_raw = sb([P, PACK, H], F32, "w2_raw")
+        nc.sync.dma_start(out=w2_raw[:], in_=w2.rearrange("(p j) c -> p j c", j=PACK))
+        nc.sync.dma_start(n2_t[:], n2)
+        mem_rows = mem.rearrange("(p t) w -> p t w", t=PACK)
+        page = [sb([P, U], F32, "page%d" % t) for t in range(PACK)]
+        for t in range(PACK):
+            nc.sync.dma_start(out=page[t][:], in_=mem_rows[:, t, :])
+        w3w_raw = sb([P, 2 * N], U8, "w3w_raw")
+        nc.sync.dma_start(out=w3w_raw[:].bitcast(I32), in_=w3_words[0].bitcast(I32))
+        w3s_raw = sb([P, N], U8, "w3s_raw")
+        nc.gpsimd.memset(w3s_raw[:].bitcast(I32), 0)
+        load_scale_rows((nc.sync, nc.sync), w3s_raw, w3_scales)
+        res_t = sb([P, PACK, U], F32, "res_t")
+        nc.sync.dma_start(out=res_t[:], in_=res.rearrange("(p t) w -> p t w", t=PACK))
+
+        sg = sb([P, S], U8, "sg")
+        nc.vector.tensor_copy(out=sg[:], in_=xs[:].indirect(offs_t[:]))
+
+        xg = sb([P, S], I32, "xg")
+        for c in range(2):
+            nc.vector.tensor_copy(
+                out=xg[:, BANK * c : BANK * (c + 1)].bitcast(U32), in_=xw[:].bitcast(U32).indirect(offs_t[:, 32 * c : 32 * (c + 1)])
+            )
+        w1_bf = sb([P, PACK, P, PACK], BF16, "w1_bf")
+        for raw, (first, last) in zip(w1_raw, W1_PIECES):
+            round_and_deal(w1_bf, raw[:], first // PACK, nc.vector.tensor_copy if last == H else nc.scalar.copy)
+        w1_codes = sb([P, H], U32, "w1_codes")
+        w1_scale = sb([P, H], U8, "w1_scale")
+        for first, last in ((0, 1), (1, 2), (2, 4)):
+            nc.vector.quantize_mx(
+                out=w1_codes[:, P * first : P * last].bitcast(FP8X4),
+                scales=w1_scale[:, P * first : P * last],
+                in_=w1_bf[:, first:last].rearrange("p t m j -> p (t m j)"),
+            )
+        y = [sb([P, S], F32, "y%d" % t) for t in range(PACK)]
+        for t in range(PACK):
+            for c in range(2):
+                cols = slice(BANK * c, BANK * (c + 1))
+                for once in range(1):
+                    acc = bank(2 * t + c, [P, BANK])
+                    nc.tensor.matmul_mx(
+                        out=acc[:],
+                        lhsT=w1_codes[:, P * t : P * (t + 1)].bitcast(FP8X4),
+                        lhsT_scale=w1_scale[:, P * t : P * (t + 1)],
+                        rhs=xg[:, cols].bitcast(FP8X4),
+                        rhs_scale=sg[:, cols],
+                        start=True,
+                        stop=True,
+                    )
+                    if t == 0 and c == 1:
+                        nc.vector.tensor_copy(out=y[t][:, cols], in_=acc[:])
+                    else:
+                        nc.scalar.copy(out=y[t][:, cols], in_=acc[:])
+
+
+        w2_bf = sb([P, PACK, P, PACK], BF16, "w2_bf")
+        w2_scale = sb([P, H], U8, "w2_scale")
+
+        def round_w2(piece):
+            round_and_deal(w2_bf, w2_raw[:, :, P * piece : P * (piece + 1)], 32 * piece)
+
+        def add_turned(sums, t, terms, opens, closes):
+            steps = [(b, term) for b in range(2) for term in terms]
+            for i, (b, term) in enumerate(steps):
+                nc.tensor.matmul(
+                    out=sums[:, b, t % 2, :],
+                    lhsT=term[:, P * b : P * (b + 1)],
+                    rhs=ident[:],
+                    is_transpose=True,
+                    start=(opens and i == 0),
+                    stop=(closes and i == len(steps) - 1),
+                )
+
+        def gather(half, t, ln, sums):
+            nc.vector.tensor_copy(
+                out=ln.rearrange("p v e -> p (v e)"), in_=y[t][:].indirect(n1_t[:, 32 * half : 32 * (half + 1)])
+            )
+            add_turned(sums, t, (ln[:, :, 0], ln[:, :, 1]), t % 2 == 0, False)
+
+        def distance(first, ln, diff, dist, sums):
+            nc.vector.tensor_tensor(out=diff, in0=ln[:, :, :, 0], in1=ln[:, :, :, 1], op=ALU.subtract)
+            nc.scalar.activation(out=dist, in_=diff, func=ACT.Abs, scale=3.0)
+            for e in range(ln.shape[1]):
+                add_turned(sums, first + e, (dist[:, e],), False, (first + e) % 2 == 1)
+
+        def turn_back(half, u, sums, back):
+            zt = sb([P, 2, P, 2], BF16, "zt%d_%d" % (half, u))
+            nc.scalar.activation(out=zt[:], in_=sums[:].rearrange("v b e p -> v b p e"), func=ACT.Copy, scale=0.25)
+            words = zt[:].rearrange("v b p e -> v (b p e)").bitcast(F32)
+            for b in range(2):
+                nc.tensor.transpose(back[:, b, u, :], words[:, P * b : P * (b + 1)], ident[:])
+
+        def interleave(half, back):
+            z_words = sb([P, 2, P, 2], F32, "z_words%d" % half)
+            nc.scalar.copy(out=z_words[:], in_=back[:].rearrange("p b u v -> p b v u"))
+            return z_words
+
+        def second_layer(half, z_words, banks):
+            z_codes = sb([P, VH], U32, "z_codes%d" % half)
+            z_scale = sb([P, VH], U8, "z_scale%d" % half)
+            nc.vector.quantize_mx(
+                out=z_codes[:].bitcast(FP8X4), scales=z_scale[:], in_=z_words[:].rearrange("p b v u -> p (b v u)").bitcast(BF16)
+            )
+            accs = []
+            for pair in range(2):
+                acc = bank(banks[pair], [P, 2, VH])
+                for e in range(2):
+                    t = 2 * pair + e
+                    nc.tensor.matmul_mx(
+                        out=acc[:, e, :],
+                        lhsT=w2_codes[:, P * t : P * (t + 1)].bitcast(FP8X4),
+                        lhsT_scale=w2_scale[:, P * t : P * (t + 1)],
+                        rhs=z_codes[:].bitcast(FP8X4),
+                        rhs_scale=z_scale[:],
+                        start=True,
+                        stop=True,
+                    )
+                accs.append(acc)
+            return accs
+
+        def work_tiles(name, planes, ln_tag=None, dist_tag=None):
+            ln = sb([P, planes, VH, 2], F32, "ln" + name, tag=ln_tag)
+            diff = sb([P, planes, VH], F32, "diff" + name)
+            dist = sb([P, planes, VH], F32, "dist" + name, tag=dist_tag)
+            return ln, diff, dist
+
+        sums_lo, sums_hi, back0 = bank(0, [P, 2, 2, P]), bank(2, [P, 2, 2, P]), bank(1, [P, 2, 2, P])
+        round_w2(0)
+        round_w2(1)
+        ln, diff, dist = work_tiles("A01", 2)
+        gather(0, 0, ln[:, 0], sums_lo)
+        gather(0, 1, ln[:, 1], sums_lo)
+        distance(0, ln[:], diff[:], dist[:], sums_lo)
+        round_w2(2)
+        ln, diff, dist = work_tiles("A2", 1)
+        gather(0, 2, ln[:, 0], sums_hi)
+        distance(2, ln[:], diff[:], dist[:], sums_hi)
+        turn_back(0, 0, sums_lo, back0)
+        ln, diff, dist = work_tiles("A3", 1)
+        gather(0, 3, ln[:, 0], sums_hi)
+
+        distance(3, ln[:], diff[:], dist[:], sums_hi)
+        round_w2(3)
+        turn_back(0, 1, sums_hi, back0)
+        z_words0 = interleave(0, back0)
+
+
+        sums_lo, sums_hi, back1 = bank(2, [P, 2, 2, P]), bank(1, [P, 2, 2, P]), bank(0, [P, 2, 2, P])
+        ln, diff, dist = work_tiles("B012", 3, "diffA2", "zt0_1")
+        for t in range(2):
+            gather(1, t, ln[:, t], sums_lo)
+        w2_codes = sb([P, H], U32, "w2_codes", tag="y0")
+        nc.vector.quantize_mx(out=w2_codes[:].bitcast(FP8X4), scales=w2_scale[:], in_=w2_bf[:].rearrange("p t m j -> p (t m j)"))
+        distance(0, ln[:, 0:2], diff[:, 0:2], dist[:, 0:2], sums_lo)
+        gather(1, 2, ln[:, 2], sums_hi)
+        accs0 = second_layer(0, z_words0, (4, 5))
+        h01 = [sb([P, 2, VH], F32, "h01_%d" % half) for half in range(2)]
+        nc.scalar.copy(out=h01[0][:], in_=accs0[0][:])
+        distance(2, ln[:, 2:3], diff[:, 2:3], dist[:, 2:3], sums_hi)
+        turn_back(1, 0, sums_lo, back1)
+        ln, diff, dist = work_tiles("B3", 1, "z_words0", "z_codes0")
+        gather(1, 3, ln[:, 0], sums_hi)
+
+        distance(3, ln[:], diff[:], dist[:], sums_hi)
+        turn_back(1, 1, sums_hi, back1)
+        z_words1 = interleave(1, back1)
+        h23 = sb([P, 2, V], F32, "h23", tag="zt1_1")
+        nc.scalar.copy(out=h23[:, :, 0:VH], in_=accs0[1][:])
+
+        def scatter(t, values, first, last):
+            nc.vector.tensor_copy(out=page[t][:].indirect(n2_t[:, first // 16 : last // 16]), in_=values)
+
+        starts = [sum(CHUNKS[:i]) for i in range(len(CHUNKS))]
+        pairs = [sb([P, 2, width, 2], BF16, "pairs%d" % i) for i, width in enumerate(CHUNKS)]
+
+        def round_page(t, i):
+            nc.scalar.copy(out=pairs[i][:, t // 2, :, t % 2], in_=page[t][:, starts[i] : starts[i] + CHUNKS[i]])
+
+        scatter(0, h01[0][:, 0, :], 0, VH)
+        scatter(1, h01[0][:, 1, :], 0, VH)
+        w3w = sb([P, PACK, P, 2], U8, "w3w", tag="h01_0")
+        w3s = sb([P, PACK, P], U8, "w3s", tag="diffB3")
+        nc.gpsimd.tensor_copy(out=w3w[:], in_=w3w_raw[:].rearrange("p (m t b) -> p t m b", t=PACK, b=2))
+        nc.gpsimd.tensor_copy(out=w3s[:], in_=w3s_raw[:].rearrange("p (m t) -> p t m", t=PACK))
+        accs1 = second_layer(1, z_words1, (6, 7))
+        nc.scalar.copy(out=h01[1][:], in_=accs1[0][:])
+        nc.scalar.copy(out=h23[:, :, VH:V], in_=accs1[1][:])
+        scatter(2, h23[:, 0, 0:VH], 0, VH)
+        scatter(0, h01[1][:, 0, :], VH, V)
+        scatter(1, h01[1][:, 1, :], VH, V)
+        scatter(2, h23[:, 0, VH:V], VH, V)
+        scatter(3, h23[:, 1, :], 0, V)
+
+        for t in range(PACK - 1):
+            for i in range(len(CHUNKS)):
+                round_page(t, i)
+
+        out_rows = out_0.rearrange("(p t) w -> p t w", t=PACK)
+        out_words = out_1[0].rearrange("p n t -> p (n t)").bitcast(I32)
+        o_scale = sb([P, U], U8, "o_scale")
+        codes, outs = {}, {}
+
+        def quantise_page(i):
+            width = CHUNKS[i]
+            round_page(PACK - 1, i)
+            z2_words = sb([P, width, 2], F32, "z2_words%d" % i)
+            join = nc.scalar.copy if i in (2, 3, 4) else nc.vector.tensor_copy
+            join(out=z2_words[:], in_=pairs[i][:].rearrange("p u w e -> p u (w e)").bitcast(F32).rearrange("p u w -> p w u"))
+            z2_codes = sb([P, width], U32, "z2_codes%d" % i)
+            z2_scale = sb([P, width], U8, "z2_scale%d" % i)
+            nc.vector.quantize_mx(
+                out=z2_codes[:].bitcast(FP8X4), scales=z2_scale[:], in_=z2_words[:].rearrange("p w u -> p (w u)").bitcast(BF16)
+            )
+            codes[i] = (z2_codes, z2_scale)
+
+        def last_layer(i):
+            width = CHUNKS[i]
+            cols = slice(starts[i], starts[i] + width)
+            z2_codes, z2_scale = codes[i]
+            o32 = sb([P, PACK, width], F32, "o32_%d" % i)
+            per_bank = BANK // width
+            for b in range(PACK // per_bank):
+                acc = bank((starts[i] // P + b) % 8, [P, per_bank, width])
+                for e in range(per_bank):
+                    t = per_bank * b + e
+                    nc.tensor.matmul_mx(
+                        out=acc[:, e, :],
+                        lhsT=w3w[:, t].rearrange("p m b -> p (m b)").bitcast(FP4X4),
+                        lhsT_scale=w3s[:, t, :],
+                        rhs=z2_codes[:].bitcast(FP8X4),
+                        rhs_scale=z2_scale[:],
+                        start=True,
+                        stop=True,
+                    )
+                rows = slice(per_bank * b, per_bank * (b + 1))
+                nc.vector.tensor_tensor(out=o32[:, rows, :], in0=acc[:], in1=res_t[:, rows, cols], op=ALU.add)
+            nc.sync.dma_start(out=out_rows[:, :, cols], in_=o32[:])
+            outs[i] = o32
+
+        def hand_on(i):
+            width = CHUNKS[i]
+            cols = slice(starts[i], starts[i] + width)
+            o_bf = sb([P, width, PACK], BF16, "o_bf%d" % i)
+            weave = nc.vector.tensor_copy if i in (len(CHUNKS) - 1,) else nc.scalar.copy
+            weave(out=o_bf[:], in_=outs[i][:].rearrange("p t w -> p w t"))
+            o_codes = sb([P, width], I32, "o_codes%d" % i)
+            nc.vector.quantize_mx(
+                out=o_codes[:].bitcast(FP8X4), scales=o_scale[:, cols], in_=o_bf[:].rearrange("p w t -> p (w t)")
+            )
+            nc.sync.dma_start(out=out_words[:, cols], in_=o_codes[:])
+
+        quantise_page(0)
+        quantise_page(1)
+        for i in range(len(CHUNKS)):
+            last_layer(i)
+            if i + 2 < len(CHUNKS):
+                quantise_page(i + 2)
+            hand_on(i)
+        for q in range(4):
+            queue = nc.scalar if q < 3 else nc.sync
+            queue.dma_start(out=out_2[0, 4 * q : 4 * q + 4, :].bitcast(I32), in_=o_scale[32 * q : 32 * q + 4, :].bitcast(I32))

@@ -21,6 +21,8 @@ P = 128
 PACK = 4
 BANK = 512
 VH = V // 2
+PIECE = 256
+CODE_STORES = (0, 640, 896, 1024)
 W1_PIECES = ((0, 256), (256, 384), (384, 512))
 CHUNKS = (128, 256, 256, 256, 128)
 
@@ -47,8 +49,8 @@ def tile_picked_deeppgappage_none_po_kernel(
         def round_and_deal(grouped, raw, m0, copy=nc.scalar.copy):
             width = raw.shape[2] // PACK
             copy(
-                out=grouped[:, :, m0 : m0 + width, :].rearrange("p t m j -> p m t j"),
-                in_=raw.rearrange("p j (m t) -> p m t j", t=PACK),
+                out=grouped[:, :, m0 : m0 + width, :].rearrange("p t m j -> p m j t"),
+                in_=raw.rearrange("p j (m t) -> p m j t", t=PACK),
             )
 
         def clock(ap, name):
@@ -60,12 +62,13 @@ def tile_picked_deeppgappage_none_po_kernel(
         n2_t = lists.tile([P, V // 16], U16, name="n2_t")
 
         xs = sb([P, T], U8, "xs")
-        nc.vector.memset(xs[:].bitcast(I32), 0)
+        nc.gpsimd.memset(xs[:].bitcast(I32), 0)
         ident = sb([P, P], F32, "ident")
         make_identity(nc, ident[:])
 
         nc.sync.dma_start(offs_t[:], offs)
-        load_scale_rows((nc.sync, nc.scalar), xs, x_scales)
+        nc.sync.dma_start(n1_t[:], n1)
+        load_scale_rows((nc.sync, nc.sync), xs, x_scales)
         xw = sb([P, T], I32, "xw")
         nc.sync.dma_start(out=xw[:], in_=x_words[0].rearrange("p n t -> p (n t)").bitcast(I32))
         w1_rows = w1.rearrange("(p j) c -> p j c", j=PACK)
@@ -74,7 +77,11 @@ def tile_picked_deeppgappage_none_po_kernel(
             raw = sb([P, PACK, last - first], F32, "w1_raw%d" % first)
             nc.sync.dma_start(out=raw[:], in_=w1_rows[:, :, first:last])
             w1_raw.append(raw)
-        nc.sync.dma_start(n1_t[:], n1)
+        w3w_raw = sb([P, 2 * N], U8, "w3w_raw")
+        nc.sync.dma_start(out=w3w_raw[:].bitcast(I32), in_=w3_words[0].bitcast(I32))
+        w3s_raw = sb([P, N], U8, "w3s_raw")
+        nc.gpsimd.memset(w3s_raw[:].bitcast(I32), 0)
+        load_scale_rows((nc.sync, nc.sync), w3s_raw, w3_scales)
         w2_raw = sb([P, PACK, H], F32, "w2_raw")
         nc.sync.dma_start(out=w2_raw[:], in_=w2.rearrange("(p j) c -> p j c", j=PACK))
         nc.sync.dma_start(n2_t[:], n2)
@@ -82,11 +89,6 @@ def tile_picked_deeppgappage_none_po_kernel(
         page = [sb([P, U], F32, "page%d" % t) for t in range(PACK)]
         for t in range(PACK):
             nc.sync.dma_start(out=page[t][:], in_=mem_rows[:, t, :])
-        w3w_raw = sb([P, 2 * N], U8, "w3w_raw")
-        nc.sync.dma_start(out=w3w_raw[:].bitcast(I32), in_=w3_words[0].bitcast(I32))
-        w3s_raw = sb([P, N], U8, "w3s_raw")
-        nc.gpsimd.memset(w3s_raw[:].bitcast(I32), 0)
-        load_scale_rows((nc.sync, nc.sync), w3s_raw, w3_scales)
         res_t = sb([P, PACK, U], F32, "res_t")
         nc.sync.dma_start(out=res_t[:], in_=res.rearrange("(p t) w -> p t w", t=PACK))
 
@@ -109,6 +111,10 @@ def tile_picked_deeppgappage_none_po_kernel(
                 scales=w1_scale[:, P * first : P * last],
                 in_=w1_bf[:, first:last].rearrange("p t m j -> p (t m j)"),
             )
+        w3w = sb([P, PACK, P, 2], U8, "w3w", tag="w1_bf")
+        w3s = sb([P, PACK, P], U8, "w3s", tag="w1_raw384")
+        nc.vector.tensor_copy(out=w3w[:], in_=w3w_raw[:].rearrange("p (m t b) -> p t m b", t=PACK, b=2))
+        nc.vector.tensor_copy(out=w3s[:], in_=w3s_raw[:].rearrange("p (m t) -> p t m", t=PACK))
         y = [sb([P, S], F32, "y%d" % t) for t in range(PACK)]
         for t in range(PACK):
             for c in range(2):
@@ -124,10 +130,7 @@ def tile_picked_deeppgappage_none_po_kernel(
                         start=True,
                         stop=True,
                     )
-                    if t == 0 and c == 1:
-                        nc.vector.tensor_copy(out=y[t][:, cols], in_=acc[:])
-                    else:
-                        nc.scalar.copy(out=y[t][:, cols], in_=acc[:])
+                    nc.scalar.copy(out=y[t][:, cols], in_=acc[:])
 
 
         w2_bf = sb([P, PACK, P, PACK], BF16, "w2_bf")
@@ -160,8 +163,8 @@ def tile_picked_deeppgappage_none_po_kernel(
             for e in range(ln.shape[1]):
                 add_turned(sums, first + e, (dist[:, e],), False, (first + e) % 2 == 1)
 
-        def turn_back(half, u, sums, back):
-            zt = sb([P, 2, P, 2], BF16, "zt%d_%d" % (half, u))
+        def turn_back(half, u, sums, back, tag=None):
+            zt = sb([P, 2, P, 2], BF16, "zt%d_%d" % (half, u), tag=tag)
             nc.scalar.activation(out=zt[:], in_=sums[:].rearrange("v b e p -> v b p e"), func=ACT.Copy, scale=0.25)
             words = zt[:].rearrange("v b p e -> v (b p e)").bitcast(F32)
             for b in range(2):
@@ -203,42 +206,40 @@ def tile_picked_deeppgappage_none_po_kernel(
 
         sums_lo, sums_hi, back0 = bank(0, [P, 2, 2, P]), bank(2, [P, 2, 2, P]), bank(1, [P, 2, 2, P])
         round_w2(0)
-        round_w2(1)
         ln, diff, dist = work_tiles("A01", 2)
         gather(0, 0, ln[:, 0], sums_lo)
         gather(0, 1, ln[:, 1], sums_lo)
         distance(0, ln[:], diff[:], dist[:], sums_lo)
-        round_w2(2)
+        round_w2(1)
         ln, diff, dist = work_tiles("A2", 1)
         gather(0, 2, ln[:, 0], sums_hi)
         distance(2, ln[:], diff[:], dist[:], sums_hi)
         turn_back(0, 0, sums_lo, back0)
+
         ln, diff, dist = work_tiles("A3", 1)
         gather(0, 3, ln[:, 0], sums_hi)
-
         distance(3, ln[:], diff[:], dist[:], sums_hi)
-        round_w2(3)
+        round_w2(2)
         turn_back(0, 1, sums_hi, back0)
+        round_w2(3)
         z_words0 = interleave(0, back0)
 
-
         sums_lo, sums_hi, back1 = bank(2, [P, 2, 2, P]), bank(1, [P, 2, 2, P]), bank(0, [P, 2, 2, P])
-        ln, diff, dist = work_tiles("B012", 3, "diffA2", "zt0_1")
+        ln, diff, dist = work_tiles("B01", 2, "diffA2", "zt0_1")
         for t in range(2):
             gather(1, t, ln[:, t], sums_lo)
-        w2_codes = sb([P, H], U32, "w2_codes", tag="y0")
+        distance(0, ln[:], diff[:], dist[:], sums_lo)
+        w2_codes = sb([P, H], U32, "w2_codes", tag=None)
         nc.vector.quantize_mx(out=w2_codes[:].bitcast(FP8X4), scales=w2_scale[:], in_=w2_bf[:].rearrange("p t m j -> p (t m j)"))
-        distance(0, ln[:, 0:2], diff[:, 0:2], dist[:, 0:2], sums_lo)
-        gather(1, 2, ln[:, 2], sums_hi)
         accs0 = second_layer(0, z_words0, (4, 5))
         h01 = [sb([P, 2, VH], F32, "h01_%d" % half) for half in range(2)]
         nc.scalar.copy(out=h01[0][:], in_=accs0[0][:])
-        distance(2, ln[:, 2:3], diff[:, 2:3], dist[:, 2:3], sums_hi)
         turn_back(1, 0, sums_lo, back1)
-        ln, diff, dist = work_tiles("B3", 1, "z_words0", "z_codes0")
-        gather(1, 3, ln[:, 0], sums_hi)
-
-        distance(3, ln[:], diff[:], dist[:], sums_hi)
+        ln, diff, dist = work_tiles("B23", 2, "z_words0")
+        for t in range(2):
+            gather(1, 2 + t, ln[:, t], sums_hi)
+        for t in range(2):
+            distance(2 + t, ln[:, t : t + 1], diff[:, t : t + 1], dist[:, t : t + 1], sums_hi)
         turn_back(1, 1, sums_hi, back1)
         z_words1 = interleave(1, back1)
         h23 = sb([P, 2, V], F32, "h23", tag="zt1_1")
@@ -255,10 +256,6 @@ def tile_picked_deeppgappage_none_po_kernel(
 
         scatter(0, h01[0][:, 0, :], 0, VH)
         scatter(1, h01[0][:, 1, :], 0, VH)
-        w3w = sb([P, PACK, P, 2], U8, "w3w", tag="h01_0")
-        w3s = sb([P, PACK, P], U8, "w3s", tag="diffB3")
-        nc.gpsimd.tensor_copy(out=w3w[:], in_=w3w_raw[:].rearrange("p (m t b) -> p t m b", t=PACK, b=2))
-        nc.gpsimd.tensor_copy(out=w3s[:], in_=w3s_raw[:].rearrange("p (m t) -> p t m", t=PACK))
         accs1 = second_layer(1, z_words1, (6, 7))
         nc.scalar.copy(out=h01[1][:], in_=accs1[0][:])
         nc.scalar.copy(out=h23[:, :, VH:V], in_=accs1[1][:])
@@ -281,7 +278,7 @@ def tile_picked_deeppgappage_none_po_kernel(
             width = CHUNKS[i]
             round_page(PACK - 1, i)
             z2_words = sb([P, width, 2], F32, "z2_words%d" % i)
-            join = nc.scalar.copy if i in (2, 3, 4) else nc.vector.tensor_copy
+            join = nc.scalar.copy if i in (3, 4) else nc.vector.tensor_copy
             join(out=z2_words[:], in_=pairs[i][:].rearrange("p u w e -> p u (w e)").bitcast(F32).rearrange("p u w -> p w u"))
             z2_codes = sb([P, width], U32, "z2_codes%d" % i)
             z2_scale = sb([P, width], U8, "z2_scale%d" % i)
@@ -311,20 +308,27 @@ def tile_picked_deeppgappage_none_po_kernel(
                     )
                 rows = slice(per_bank * b, per_bank * (b + 1))
                 nc.vector.tensor_tensor(out=o32[:, rows, :], in0=acc[:], in1=res_t[:, rows, cols], op=ALU.add)
-            nc.sync.dma_start(out=out_rows[:, :, cols], in_=o32[:])
+                nc.sync.dma_start(out=out_rows[:, rows, cols], in_=o32[:, rows, :])
             outs[i] = o32
 
+        o_codes = sb([P, U], I32, "o_codes")
+
         def hand_on(i):
-            width = CHUNKS[i]
-            cols = slice(starts[i], starts[i] + width)
-            o_bf = sb([P, width, PACK], BF16, "o_bf%d" % i)
-            weave = nc.vector.tensor_copy if i in (len(CHUNKS) - 1,) else nc.scalar.copy
-            weave(out=o_bf[:], in_=outs[i][:].rearrange("p t w -> p w t"))
-            o_codes = sb([P, width], I32, "o_codes%d" % i)
-            nc.vector.quantize_mx(
-                out=o_codes[:].bitcast(FP8X4), scales=o_scale[:, cols], in_=o_bf[:].rearrange("p w t -> p (w t)")
-            )
-            nc.sync.dma_start(out=out_words[:, cols], in_=o_codes[:])
+            for first in range(0, CHUNKS[i], PIECE):
+                width = min(PIECE, CHUNKS[i])
+                cols = slice(starts[i] + first, starts[i] + first + width)
+                o_bf = sb([P, width, PACK], BF16, "o_bf%d" % cols.start)
+                weave = nc.vector.tensor_copy if cols.start in (896,) else nc.scalar.copy
+                weave(
+                    out=o_bf[:].rearrange("p (c i) t -> p c t i", i=4),
+                    in_=outs[i][:, :, first : first + width].rearrange("p t (c i) -> p c t i", i=4),
+                )
+                nc.vector.quantize_mx(
+                    out=o_codes[:, cols].bitcast(FP8X4), scales=o_scale[:, cols], in_=o_bf[:].rearrange("p w t -> p (w t)")
+                )
+                if cols.stop in CODE_STORES:
+                    stored = slice(CODE_STORES[CODE_STORES.index(cols.stop) - 1], cols.stop)
+                    nc.sync.dma_start(out=out_words[:, stored], in_=o_codes[:, stored])
 
         quantise_page(0)
         quantise_page(1)

@@ -20,11 +20,15 @@ ACT = mybir.ActivationFunctionType
 P = 128
 PACK = 4
 BANK = 512
+BANKS = 8
+LIST_ROWS = 16
 VH = V // 2
-PIECE = 256
-CODE_STORES = (0, 640, 896, 1024)
-W1_PIECES = ((0, 256), (256, 384), (384, 512))
+W1_SPLIT = 56
+W2_PIECES = 4
 CHUNKS = (128, 256, 256, 256, 128)
+SCALAR_CHUNKS = 2
+VECTOR_JOINS = 3
+CODE_STORES = (0, 640, 896, 1024)
 
 
 def tile_picked_deeppgappage_none_po_kernel(
@@ -42,24 +46,21 @@ def tile_picked_deeppgappage_none_po_kernel(
         def bank(number, shape):
             return psum.tile(shape, F32, name="bank%d" % number)
 
-        def load_scale_rows(queues, plane, rows):
+        def load_scale_rows(tile, rows):
             for q in range(4):
-                queues[q % 2].dma_start(out=plane[32 * q : 32 * q + 4, :].bitcast(I32), in_=rows[0, 4 * q : 4 * q + 4, :].bitcast(I32))
+                nc.sync.dma_start(out=tile[32 * q : 32 * q + 4, :].bitcast(I32), in_=rows[0, 4 * q : 4 * q + 4, :].bitcast(I32))
 
-        def round_and_deal(grouped, raw, m0, copy=nc.scalar.copy):
-            width = raw.shape[2] // PACK
-            copy(
-                out=grouped[:, :, m0 : m0 + width, :].rearrange("p t m j -> p m j t"),
-                in_=raw.rearrange("p j (m t) -> p m j t", t=PACK),
+        def quantise(codes, scale, values):
+            nc.vector.quantize_mx(out=codes.bitcast(FP8X4), scales=scale, in_=values)
+
+        def multiply(acc, weights, weights_scale, codes, scale):
+            nc.tensor.matmul_mx(
+                out=acc, lhsT=weights, lhsT_scale=weights_scale, rhs=codes.bitcast(FP8X4), rhs_scale=scale, start=True, stop=True
             )
 
-        def clock(ap, name):
-            tick = sb([P, 1], ap.dtype, name)
-            nc.gpsimd.tensor_copy(out=tick[:], in_=ap)
-
-        offs_t = lists.tile([P, S // 16], U16, name="offs_t")
-        n1_t = lists.tile([P, S // 16], U16, name="n1_t")
-        n2_t = lists.tile([P, V // 16], U16, name="n2_t")
+        offs_t = lists.tile([P, S // LIST_ROWS], U16, name="offs_t")
+        n1_t = lists.tile([P, S // LIST_ROWS], U16, name="n1_t")
+        n2_t = lists.tile([P, V // LIST_ROWS], U16, name="n2_t")
 
         xs = sb([P, T], U8, "xs")
         nc.gpsimd.memset(xs[:].bitcast(I32), 0)
@@ -68,23 +69,21 @@ def tile_picked_deeppgappage_none_po_kernel(
 
         nc.sync.dma_start(offs_t[:], offs)
         nc.sync.dma_start(n1_t[:], n1)
-        load_scale_rows((nc.sync, nc.sync), xs, x_scales)
+        load_scale_rows(xs, x_scales)
         xw = sb([P, T], I32, "xw")
         nc.sync.dma_start(out=xw[:], in_=x_words[0].rearrange("p n t -> p (n t)").bitcast(I32))
         w1_rows = w1.rearrange("(p j) c -> p j c", j=PACK)
-        w1_raw = []
-        for first, last in W1_PIECES:
-            raw = sb([P, PACK, last - first], F32, "w1_raw%d" % first)
-            nc.sync.dma_start(out=raw[:], in_=w1_rows[:, :, first:last])
-            w1_raw.append(raw)
-        w3w_raw = sb([P, 2 * N], U8, "w3w_raw")
-        nc.sync.dma_start(out=w3w_raw[:].bitcast(I32), in_=w3_words[0].bitcast(I32))
+        w1_raw = [sb([P, 2, H], F32, "w1_raw%d" % u) for u in range(2)]
+        for u in range(2):
+            nc.sync.dma_start(out=w1_raw[u][:], in_=w1_rows[:, 2 * u : 2 * u + 2, :])
         w3s_raw = sb([P, N], U8, "w3s_raw")
         nc.gpsimd.memset(w3s_raw[:].bitcast(I32), 0)
-        load_scale_rows((nc.sync, nc.sync), w3s_raw, w3_scales)
         w2_raw = sb([P, PACK, H], F32, "w2_raw")
         nc.sync.dma_start(out=w2_raw[:], in_=w2.rearrange("(p j) c -> p j c", j=PACK))
         nc.sync.dma_start(n2_t[:], n2)
+        load_scale_rows(w3s_raw, w3_scales)
+        w3w_raw = sb([P, 2 * N], U8, "w3w_raw")
+        nc.sync.dma_start(out=w3w_raw[:].bitcast(I32), in_=w3_words[0].bitcast(I32))
         mem_rows = mem.rearrange("(p t) w -> p t w", t=PACK)
         page = [sb([P, U], F32, "page%d" % t) for t in range(PACK)]
         for t in range(PACK):
@@ -94,50 +93,47 @@ def tile_picked_deeppgappage_none_po_kernel(
 
         sg = sb([P, S], U8, "sg")
         nc.vector.tensor_copy(out=sg[:], in_=xs[:].indirect(offs_t[:]))
-
         xg = sb([P, S], I32, "xg")
-        for c in range(2):
-            nc.vector.tensor_copy(
-                out=xg[:, BANK * c : BANK * (c + 1)].bitcast(U32), in_=xw[:].bitcast(U32).indirect(offs_t[:, 32 * c : 32 * (c + 1)])
-            )
+        for first in range(0, S, BANK):
+            picked = xw[:].bitcast(U32).indirect(offs_t[:, first // LIST_ROWS : (first + BANK) // LIST_ROWS])
+            nc.vector.tensor_copy(out=xg[:, first : first + BANK].bitcast(U32), in_=picked)
+
         w1_bf = sb([P, PACK, P, PACK], BF16, "w1_bf")
-        for raw, (first, last) in zip(w1_raw, W1_PIECES):
-            round_and_deal(w1_bf, raw[:], first // PACK, nc.vector.tensor_copy if last == H else nc.scalar.copy)
+        low, high = slice(0, W1_SPLIT), slice(W1_SPLIT, P)
+        for copy, walk, u, ms in (
+            (nc.gpsimd.tensor_copy, "p t m j", 0, low),
+            (nc.scalar.copy, "p m t j", 0, high),
+            (nc.scalar.copy, "p m t j", 1, low),
+            (nc.vector.tensor_copy, "p m t j", 1, high),
+        ):
+            copy(
+                out=w1_bf[:, :, ms, 2 * u : 2 * u + 2].rearrange("p t m j -> " + walk),
+                in_=w1_raw[u][:, :, PACK * ms.start : PACK * ms.stop].rearrange("p j (m t) -> " + walk, t=PACK),
+            )
         w1_codes = sb([P, H], U32, "w1_codes")
         w1_scale = sb([P, H], U8, "w1_scale")
-        for first, last in ((0, 1), (1, 2), (2, 4)):
-            nc.vector.quantize_mx(
-                out=w1_codes[:, P * first : P * last].bitcast(FP8X4),
-                scales=w1_scale[:, P * first : P * last],
-                in_=w1_bf[:, first:last].rearrange("p t m j -> p (t m j)"),
-            )
-        w3w = sb([P, PACK, P, 2], U8, "w3w", tag="w1_bf")
-        w3s = sb([P, PACK, P], U8, "w3s", tag="w1_raw384")
-        nc.vector.tensor_copy(out=w3w[:], in_=w3w_raw[:].rearrange("p (m t b) -> p t m b", t=PACK, b=2))
-        nc.vector.tensor_copy(out=w3s[:], in_=w3s_raw[:].rearrange("p (m t) -> p t m", t=PACK))
-        y = [sb([P, S], F32, "y%d" % t) for t in range(PACK)]
-        for t in range(PACK):
-            for c in range(2):
-                cols = slice(BANK * c, BANK * (c + 1))
-                for once in range(1):
-                    acc = bank(2 * t + c, [P, BANK])
-                    nc.tensor.matmul_mx(
-                        out=acc[:],
-                        lhsT=w1_codes[:, P * t : P * (t + 1)].bitcast(FP8X4),
-                        lhsT_scale=w1_scale[:, P * t : P * (t + 1)],
-                        rhs=xg[:, cols].bitcast(FP8X4),
-                        rhs_scale=sg[:, cols],
-                        start=True,
-                        stop=True,
-                    )
-                    nc.scalar.copy(out=y[t][:, cols], in_=acc[:])
+        for first, last in ((0, 1), (1, 2), (2, PACK)):
+            cols = slice(P * first, P * last)
+            quantise(w1_codes[:, cols], w1_scale[:, cols], w1_bf[:, first:last].rearrange("p t m j -> p (t m j)"))
 
+        y = [sb([P, S], F32, "y%d" % t) for t in range(PACK)]
+        pieces = [(0, first, BANK // 2) for first in range(0, S, BANK // 2)]
+        pieces = pieces + [(t, first, BANK) for t in range(1, PACK) for first in range(0, S, BANK)]
+        for number, (t, first, width) in enumerate(pieces):
+            cols, dealt = slice(first, first + width), slice(P * t, P * (t + 1))
+            acc = bank(number % BANKS, [P, width])
+            multiply(acc[:], w1_codes[:, dealt].bitcast(FP8X4), w1_scale[:, dealt], xg[:, cols], sg[:, cols])
+            copy = nc.vector.tensor_copy if t == 0 and number % 2 == 1 else nc.scalar.copy
+            copy(out=y[t][:, cols], in_=acc[:])
 
         w2_bf = sb([P, PACK, P, PACK], BF16, "w2_bf")
         w2_scale = sb([P, H], U8, "w2_scale")
-
-        def round_w2(piece):
-            round_and_deal(w2_bf, w2_raw[:, :, P * piece : P * (piece + 1)], 32 * piece)
+        for piece in range(W2_PIECES):
+            copy, walk = (nc.scalar.copy, "p m j t") if piece == W2_PIECES - 1 else (nc.gpsimd.tensor_copy, "p t m j")
+            copy(
+                out=w2_bf[:, :, 32 * piece : 32 * (piece + 1), :].rearrange("p t m j -> " + walk),
+                in_=w2_raw[:, :, P * piece : P * (piece + 1)].rearrange("p j (m t) -> " + walk, t=PACK),
+            )
 
         def add_turned(sums, t, terms, opens, closes):
             steps = [(b, term) for b in range(2) for term in terms]
@@ -152,13 +148,12 @@ def tile_picked_deeppgappage_none_po_kernel(
                 )
 
         def gather(half, t, ln, sums):
-            nc.vector.tensor_copy(
-                out=ln.rearrange("p v e -> p (v e)"), in_=y[t][:].indirect(n1_t[:, 32 * half : 32 * (half + 1)])
-            )
+            entries = n1_t[:, half * 2 * VH // LIST_ROWS : (half + 1) * 2 * VH // LIST_ROWS]
+            nc.vector.tensor_copy(out=ln.rearrange("p v e -> p (v e)"), in_=y[t][:].indirect(entries))
             add_turned(sums, t, (ln[:, :, 0], ln[:, :, 1]), t % 2 == 0, False)
 
-        def distance(first, ln, diff, dist, sums):
-            nc.vector.tensor_tensor(out=diff, in0=ln[:, :, :, 0], in1=ln[:, :, :, 1], op=ALU.subtract)
+        def distance(first, ln, diff, dist, sums, engine):
+            engine.tensor_tensor(out=diff, in0=ln[:, :, :, 0], in1=ln[:, :, :, 1], op=ALU.subtract)
             nc.scalar.activation(out=dist, in_=diff, func=ACT.Abs, scale=3.0)
             for e in range(ln.shape[1]):
                 add_turned(sums, first + e, (dist[:, e],), False, (first + e) % 2 == 1)
@@ -178,24 +173,13 @@ def tile_picked_deeppgappage_none_po_kernel(
         def second_layer(half, z_words, banks):
             z_codes = sb([P, VH], U32, "z_codes%d" % half)
             z_scale = sb([P, VH], U8, "z_scale%d" % half)
-            nc.vector.quantize_mx(
-                out=z_codes[:].bitcast(FP8X4), scales=z_scale[:], in_=z_words[:].rearrange("p b v u -> p (b v u)").bitcast(BF16)
-            )
-            accs = []
-            for pair in range(2):
-                acc = bank(banks[pair], [P, 2, VH])
+            quantise(z_codes[:], z_scale[:], z_words[:].rearrange("p b v u -> p (b v u)").bitcast(BF16))
+            accs = {}
+            for u in banks:
+                accs[u] = bank(banks[u], [P, 2, VH])
                 for e in range(2):
-                    t = 2 * pair + e
-                    nc.tensor.matmul_mx(
-                        out=acc[:, e, :],
-                        lhsT=w2_codes[:, P * t : P * (t + 1)].bitcast(FP8X4),
-                        lhsT_scale=w2_scale[:, P * t : P * (t + 1)],
-                        rhs=z_codes[:].bitcast(FP8X4),
-                        rhs_scale=z_scale[:],
-                        start=True,
-                        stop=True,
-                    )
-                accs.append(acc)
+                    dealt = slice(P * (2 * u + e), P * (2 * u + e + 1))
+                    multiply(accs[u][:, e, :], w2_codes[:, dealt].bitcast(FP8X4), w2_scale[:, dealt], z_codes[:], z_scale[:])
             return accs
 
         def work_tiles(name, planes, ln_tag=None, dist_tag=None):
@@ -204,131 +188,116 @@ def tile_picked_deeppgappage_none_po_kernel(
             dist = sb([P, planes, VH], F32, "dist" + name, tag=dist_tag)
             return ln, diff, dist
 
-        sums_lo, sums_hi, back0 = bank(0, [P, 2, 2, P]), bank(2, [P, 2, 2, P]), bank(1, [P, 2, 2, P])
-        round_w2(0)
-        ln, diff, dist = work_tiles("A01", 2)
-        gather(0, 0, ln[:, 0], sums_lo)
-        gather(0, 1, ln[:, 1], sums_lo)
-        distance(0, ln[:], diff[:], dist[:], sums_lo)
-        round_w2(1)
-        ln, diff, dist = work_tiles("A2", 1)
-        gather(0, 2, ln[:, 0], sums_hi)
-        distance(2, ln[:], diff[:], dist[:], sums_hi)
-        turn_back(0, 0, sums_lo, back0)
-
-        ln, diff, dist = work_tiles("A3", 1)
-        gather(0, 3, ln[:, 0], sums_hi)
-        distance(3, ln[:], diff[:], dist[:], sums_hi)
-        round_w2(2)
-        turn_back(0, 1, sums_hi, back0)
-        round_w2(3)
-        z_words0 = interleave(0, back0)
-
-        sums_lo, sums_hi, back1 = bank(2, [P, 2, 2, P]), bank(1, [P, 2, 2, P]), bank(0, [P, 2, 2, P])
-        ln, diff, dist = work_tiles("B01", 2, "diffA2", "zt0_1")
+        sums_lo, sums_hi, back_a = bank(2, [P, 2, 2, P]), bank(3, [P, 2, 2, P]), bank(1, [P, 2, 2, P])
+        ln_a01, diff_a01, dist_a01 = work_tiles("A01", 2)
         for t in range(2):
-            gather(1, t, ln[:, t], sums_lo)
-        distance(0, ln[:], diff[:], dist[:], sums_lo)
-        w2_codes = sb([P, H], U32, "w2_codes", tag=None)
-        nc.vector.quantize_mx(out=w2_codes[:].bitcast(FP8X4), scales=w2_scale[:], in_=w2_bf[:].rearrange("p t m j -> p (t m j)"))
-        accs0 = second_layer(0, z_words0, (4, 5))
+            gather(0, t, ln_a01[:, t], sums_lo)
+        distance(0, ln_a01[:], diff_a01[:], dist_a01[:], sums_lo, nc.gpsimd)
+        tiles_a = {t: work_tiles("A%d" % t, 1) for t in (2, 3)}
+        for t in (2, 3):
+            gather(0, t, tiles_a[t][0][:, 0], sums_hi)
+        for t in (2, 3):
+            distance(t, tiles_a[t][0][:], tiles_a[t][1][:], tiles_a[t][2][:], sums_hi, nc.gpsimd)
+        turn_back(0, 0, sums_lo, back_a, "diffA3")
+        turn_back(0, 1, sums_hi, back_a)
+        z_words_a = interleave(0, back_a)
+
+        sums_lo, sums_hi, back_b = bank(3, [P, 2, 2, P]), bank(1, [P, 2, 2, P]), bank(0, [P, 2, 2, P])
+        ln_b, diff_b, dist_b = work_tiles("B012", 3, "diffA01", "zt0_1")
+        for t in range(3):
+            gather(1, t, ln_b[:, t], sums_lo if t < 2 else sums_hi)
+        w2_codes = sb([P, H], U32, "w2_codes", tag="y2")
+        quantise(w2_codes[:], w2_scale[:], w2_bf[:].rearrange("p t m j -> p (t m j)"))
+        accs_a = second_layer(0, z_words_a, {0: 4, 1: 5})
         h01 = [sb([P, 2, VH], F32, "h01_%d" % half) for half in range(2)]
-        nc.scalar.copy(out=h01[0][:], in_=accs0[0][:])
-        turn_back(1, 0, sums_lo, back1)
-        ln, diff, dist = work_tiles("B23", 2, "z_words0")
-        for t in range(2):
-            gather(1, 2 + t, ln[:, t], sums_hi)
-        for t in range(2):
-            distance(2 + t, ln[:, t : t + 1], diff[:, t : t + 1], dist[:, t : t + 1], sums_hi)
-        turn_back(1, 1, sums_hi, back1)
-        z_words1 = interleave(1, back1)
-        h23 = sb([P, 2, V], F32, "h23", tag="zt1_1")
-        nc.scalar.copy(out=h23[:, :, 0:VH], in_=accs0[1][:])
+        nc.scalar.copy(out=h01[0][:], in_=accs_a[0][:])
+        distance(0, ln_b[:, 0:2], diff_b[:, 0:2], dist_b[:, 0:2], sums_lo, nc.gpsimd)
+        late = sb([P, 3, VH], F32, "late", tag="z_words0")
+        ln_b3 = late[:, 0:2].rearrange("p a (b e) -> p (a b) e", e=2)
+        gather(1, 3, ln_b3, sums_hi)
+        distance(2, ln_b[:, 2:3], late[:, 2:3], dist_b[:, 2:3], sums_hi, nc.gpsimd)
+        turn_back(1, 0, sums_lo, back_b)
+        h2_a = sb([P, VH], F32, "h2_a")
+        nc.scalar.copy(out=h2_a[:], in_=accs_a[1][:, 0])
+        dist_b3 = sb([P, 1, VH], F32, "dist_b3")
+        distance(3, ln_b3.unsqueeze(1), diff_b[:, 2:3], dist_b3[:], sums_hi, nc.vector)
 
-        def scatter(t, values, first, last):
-            nc.vector.tensor_copy(out=page[t][:].indirect(n2_t[:, first // 16 : last // 16]), in_=values)
+        w3w = sb([P, PACK, P, 2], U8, "w3w", tag="z_words0")
+        w3s = sb([P, PACK, P], U8, "w3s", tag="diffB012")
+        nc.gpsimd.tensor_copy(out=w3w[:], in_=w3w_raw[:].rearrange("p (m t b) -> p t m b", t=PACK, b=2))
+        nc.gpsimd.tensor_copy(out=w3s[:], in_=w3s_raw[:].rearrange("p (m t) -> p t m", t=PACK))
+        turn_back(1, 1, sums_hi, back_b)
+        z_words_b = interleave(1, back_b)
+        h3_a = sb([P, VH], F32, "h3_a", tag="zt1_1")
+        nc.scalar.copy(out=h3_a[:], in_=accs_a[1][:, 1])
+
+        def scatter(half, t, values):
+            entries = n2_t[:, half * VH // LIST_ROWS : (half + 1) * VH // LIST_ROWS]
+            nc.vector.tensor_copy(out=page[t][:].indirect(entries), in_=values)
 
         starts = [sum(CHUNKS[:i]) for i in range(len(CHUNKS))]
         pairs = [sb([P, 2, width, 2], BF16, "pairs%d" % i) for i, width in enumerate(CHUNKS)]
 
         def round_page(t, i):
-            nc.scalar.copy(out=pairs[i][:, t // 2, :, t % 2], in_=page[t][:, starts[i] : starts[i] + CHUNKS[i]])
+            copy = nc.gpsimd.tensor_copy if t < 2 and i >= SCALAR_CHUNKS else nc.scalar.copy
+            copy(out=pairs[i][:, t // 2, :, t % 2], in_=page[t][:, starts[i] : starts[i] + CHUNKS[i]])
 
-        scatter(0, h01[0][:, 0, :], 0, VH)
-        scatter(1, h01[0][:, 1, :], 0, VH)
-        accs1 = second_layer(1, z_words1, (6, 7))
-        nc.scalar.copy(out=h01[1][:], in_=accs1[0][:])
-        nc.scalar.copy(out=h23[:, :, VH:V], in_=accs1[1][:])
-        scatter(2, h23[:, 0, 0:VH], 0, VH)
-        scatter(0, h01[1][:, 0, :], VH, V)
-        scatter(1, h01[1][:, 1, :], VH, V)
-        scatter(2, h23[:, 0, VH:V], VH, V)
-        scatter(3, h23[:, 1, :], 0, V)
-
-        for t in range(PACK - 1):
+        scatter(0, 0, h01[0][:, 0, :])
+        scatter(0, 1, h01[0][:, 1, :])
+        scatter(0, 2, h2_a[:])
+        accs_b = second_layer(1, z_words_b, {1: 7, 0: 6})
+        h2_b = sb([P, VH], F32, "h2_b")
+        h3_b = sb([P, VH], F32, "h3_b", tag="z_codes1")
+        nc.scalar.copy(out=h2_b[:], in_=accs_b[1][:, 0])
+        nc.scalar.copy(out=h01[1][:], in_=accs_b[0][:])
+        nc.scalar.copy(out=h3_b[:], in_=accs_b[1][:, 1])
+        scatter(0, 3, h3_a[:])
+        scatter(1, 2, h2_b[:])
+        scatter(1, 0, h01[1][:, 0, :])
+        scatter(1, 1, h01[1][:, 1, :])
+        scatter(1, 3, h3_b[:])
+        for t in (2, 0, 1):
             for i in range(len(CHUNKS)):
                 round_page(t, i)
 
         out_rows = out_0.rearrange("(p t) w -> p t w", t=PACK)
         out_words = out_1[0].rearrange("p n t -> p (n t)").bitcast(I32)
         o_scale = sb([P, U], U8, "o_scale")
-        codes, outs = {}, {}
+        z2_mx, o32 = {}, {}
 
         def quantise_page(i):
-            width = CHUNKS[i]
             round_page(PACK - 1, i)
-            z2_words = sb([P, width, 2], F32, "z2_words%d" % i)
-            join = nc.scalar.copy if i in (3, 4) else nc.vector.tensor_copy
+            z2_words = sb([P, CHUNKS[i], 2], F32, "z2_words%d" % i)
+            join = nc.vector.tensor_copy if i < VECTOR_JOINS else nc.scalar.copy
             join(out=z2_words[:], in_=pairs[i][:].rearrange("p u w e -> p u (w e)").bitcast(F32).rearrange("p u w -> p w u"))
-            z2_codes = sb([P, width], U32, "z2_codes%d" % i)
-            z2_scale = sb([P, width], U8, "z2_scale%d" % i)
-            nc.vector.quantize_mx(
-                out=z2_codes[:].bitcast(FP8X4), scales=z2_scale[:], in_=z2_words[:].rearrange("p w u -> p (w u)").bitcast(BF16)
-            )
-            codes[i] = (z2_codes, z2_scale)
+            z2_mx[i] = (sb([P, CHUNKS[i]], U32, "z2_codes%d" % i), sb([P, CHUNKS[i]], U8, "z2_scale%d" % i))
+            quantise(z2_mx[i][0][:], z2_mx[i][1][:], z2_words[:].rearrange("p w u -> p (w u)").bitcast(BF16))
 
         def last_layer(i):
-            width = CHUNKS[i]
-            cols = slice(starts[i], starts[i] + width)
-            z2_codes, z2_scale = codes[i]
-            o32 = sb([P, PACK, width], F32, "o32_%d" % i)
-            per_bank = BANK // width
+            cols = slice(starts[i], starts[i] + CHUNKS[i])
+            o32[i] = sb([P, PACK, CHUNKS[i]], F32, "o32_%d" % i)
+            per_bank = BANK // CHUNKS[i]
             for b in range(PACK // per_bank):
-                acc = bank((starts[i] // P + b) % 8, [P, per_bank, width])
+                acc = bank(starts[i] // P + b, [P, per_bank, CHUNKS[i]])
                 for e in range(per_bank):
                     t = per_bank * b + e
-                    nc.tensor.matmul_mx(
-                        out=acc[:, e, :],
-                        lhsT=w3w[:, t].rearrange("p m b -> p (m b)").bitcast(FP4X4),
-                        lhsT_scale=w3s[:, t, :],
-                        rhs=z2_codes[:].bitcast(FP8X4),
-                        rhs_scale=z2_scale[:],
-                        start=True,
-                        stop=True,
-                    )
-                rows = slice(per_bank * b, per_bank * (b + 1))
-                nc.vector.tensor_tensor(out=o32[:, rows, :], in0=acc[:], in1=res_t[:, rows, cols], op=ALU.add)
-                nc.sync.dma_start(out=out_rows[:, rows, cols], in_=o32[:, rows, :])
-            outs[i] = o32
+                    weights = w3w[:, t].rearrange("p m b -> p (m b)").bitcast(FP4X4)
+                    multiply(acc[:, e, :], weights, w3s[:, t, :], z2_mx[i][0][:], z2_mx[i][1][:])
+                planes = slice(per_bank * b, per_bank * (b + 1))
+                nc.vector.tensor_tensor(out=o32[i][:, planes, :], in0=acc[:], in1=res_t[:, planes, cols], op=ALU.add)
+                nc.sync.dma_start(out=out_rows[:, planes, cols], in_=o32[i][:, planes, :])
 
         o_codes = sb([P, U], I32, "o_codes")
 
         def hand_on(i):
-            for first in range(0, CHUNKS[i], PIECE):
-                width = min(PIECE, CHUNKS[i])
-                cols = slice(starts[i] + first, starts[i] + first + width)
-                o_bf = sb([P, width, PACK], BF16, "o_bf%d" % cols.start)
-                weave = nc.vector.tensor_copy if cols.start in (896,) else nc.scalar.copy
-                weave(
-                    out=o_bf[:].rearrange("p (c i) t -> p c t i", i=4),
-                    in_=outs[i][:, :, first : first + width].rearrange("p t (c i) -> p c t i", i=4),
-                )
-                nc.vector.quantize_mx(
-                    out=o_codes[:, cols].bitcast(FP8X4), scales=o_scale[:, cols], in_=o_bf[:].rearrange("p w t -> p (w t)")
-                )
-                if cols.stop in CODE_STORES:
-                    stored = slice(CODE_STORES[CODE_STORES.index(cols.stop) - 1], cols.stop)
-                    nc.sync.dma_start(out=out_words[:, stored], in_=o_codes[:, stored])
+            cols = slice(starts[i], starts[i] + CHUNKS[i])
+            o_bf = sb([P, CHUNKS[i], PACK], BF16, "o_bf%d" % i)
+            weave = nc.vector.tensor_copy if i == len(CHUNKS) - 1 else nc.scalar.copy
+            weave(out=o_bf[:].rearrange("p (c n) t -> p c t n", n=4), in_=o32[i][:].rearrange("p t (c n) -> p c t n", n=4))
+            quantise(o_codes[:, cols], o_scale[:, cols], o_bf[:].rearrange("p w t -> p (w t)"))
+            if cols.stop in CODE_STORES:
+                stored = slice(CODE_STORES[CODE_STORES.index(cols.stop) - 1], cols.stop)
+                nc.sync.dma_start(out=out_words[:, stored], in_=o_codes[:, stored])
 
         quantise_page(0)
         quantise_page(1)

from contextlib import ExitStack

import concourse.mybir as mybir
from concourse.masks import make_identity

K, T, S, V, N, H, U = 512, 2048, 1024, 512, 512, 512, 1024
FLOPS = 2 * K * H * S + 2 * H * H * V + 2 * H * N * U

F32 = mybir.dt.float32
BF16 = mybir.dt.bfloat16
I32 = mybir.dt.int32
U32 = mybir.dt.uint32
U16 = mybir.dt.uint16
U8 = mybir.dt.uint8
FP8X4 = mybir.dt.float8_e4m3fn_x4
FP4X4 = mybir.dt.float4_e2m1fn_x4
ALU = mybir.AluOpType
ACT = mybir.ActivationFunctionType

P = 128
PACK = 4
BANK = 512
BANKS = 8
LIST_ROWS = 16
VH = V // 2
W1_SPLIT = 56
W2_PIECES = 4
CHUNKS = (128, 256, 256, 256, 128)
SCALAR_CHUNKS = 2
VECTOR_JOINS = 3
CODE_STORES = (0, 640, 896, 1024)


def tile_picked_deeppgappage_none_po_kernel(
    tc, x_words, x_scales, w1, w2, mem, w3_words, w3_scales, res, offs, n1, n2, out_0, out_1, out_2
):
    nc = tc.nc
    with ExitStack() as ctx:
        lists = ctx.enter_context(tc.tile_pool(name="lists", bufs=1))
        keep = ctx.enter_context(tc.tile_pool(name="keep", bufs=1))
        psum = ctx.enter_context(tc.psum_pool(name="psum", bufs=1))

        def sb(shape, dtype, name, tag=None):
            return keep.tile(shape, dtype, name=name, tag=tag or name, align_bytes=64)

        def bank(number, shape):
            return psum.tile(shape, F32, name="bank%d" % number)

        def load_scale_rows(tile, rows):
            for q in range(4):
                nc.sync.dma_start(out=tile[32 * q : 32 * q + 4, :].bitcast(I32), in_=rows[0, 4 * q : 4 * q + 4, :].bitcast(I32))

        def quantise(codes, scale, values):
            nc.vector.quantize_mx(out=codes.bitcast(FP8X4), scales=scale, in_=values)

        def multiply(acc, weights, weights_scale, codes, scale):
            nc.tensor.matmul_mx(
                out=acc, lhsT=weights, lhsT_scale=weights_scale, rhs=codes.bitcast(FP8X4), rhs_scale=scale, start=True, stop=True
            )

        offs_t = lists.tile([P, S // LIST_ROWS], U16, name="offs_t")
        n1_t = lists.tile([P, S // LIST_ROWS], U16, name="n1_t")
        n2_t = lists.tile([P, V // LIST_ROWS], U16, name="n2_t")

        xs = sb([P, T], U8, "xs")
        nc.gpsimd.memset(xs[:].bitcast(I32), 0)
        ident = sb([P, P], F32, "ident")
        make_identity(nc, ident[:])

        nc.sync.dma_start(offs_t[:], offs)
        nc.sync.dma_start(n1_t[:], n1)
        load_scale_rows(xs, x_scales)
        xw = sb([P, T], I32, "xw")
        nc.sync.dma_start(out=xw[:], in_=x_words[0].rearrange("p n t -> p (n t)").bitcast(I32))
        w1_rows = w1.rearrange("(p j) c -> p j c", j=PACK)
        w1_raw = [sb([P, 2, H], F32, "w1_raw%d" % u) for u in range(2)]
        for u in range(2):
            nc.sync.dma_start(out=w1_raw[u][:], in_=w1_rows[:, 2 * u : 2 * u + 2, :])
        w3s_raw = sb([P, N], U8, "w3s_raw")
        nc.gpsimd.memset(w3s_raw[:].bitcast(I32), 0)
        w2_raw = sb([P, PACK, H], F32, "w2_raw")
        nc.sync.dma_start(out=w2_raw[:], in_=w2.rearrange("(p j) c -> p j c", j=PACK))
        nc.sync.dma_start(n2_t[:], n2)
        load_scale_rows(w3s_raw, w3_scales)
        w3w_raw = sb([P, 2 * N], U8, "w3w_raw")
        nc.sync.dma_start(out=w3w_raw[:].bitcast(I32), in_=w3_words[0].bitcast(I32))
        mem_rows = mem.rearrange("(p t) w -> p t w", t=PACK)
        page = [sb([P, U], F32, "page%d" % t) for t in range(PACK)]
        for t in range(PACK):
            nc.sync.dma_start(out=page[t][:], in_=mem_rows[:, t, :])
        res_t = sb([P, PACK, U], F32, "res_t")
        nc.sync.dma_start(out=res_t[:], in_=res.rearrange("(p t) w -> p t w", t=PACK))

        sg = sb([P, S], U8, "sg")
        nc.vector.tensor_copy(out=sg[:], in_=xs[:].indirect(offs_t[:]))
        xg = sb([P, S], I32, "xg")
        for first in range(0, S, BANK):
            picked = xw[:].bitcast(U32).indirect(offs_t[:, first // LIST_ROWS : (first + BANK) // LIST_ROWS])
            nc.vector.tensor_copy(out=xg[:, first : first + BANK].bitcast(U32), in_=picked)

        w1_bf = sb([P, PACK, P, PACK], BF16, "w1_bf")
        low, high = slice(0, W1_SPLIT), slice(W1_SPLIT, P)
        for copy, walk, u, ms in (
            (nc.gpsimd.tensor_copy, "p t m j", 0, low),
            (nc.scalar.copy, "p m t j", 0, high),
            (nc.scalar.copy, "p m t j", 1, low),
            (nc.vector.tensor_copy, "p m t j", 1, high),
        ):
            copy(
                out=w1_bf[:, :, ms, 2 * u : 2 * u + 2].rearrange("p t m j -> " + walk),
                in_=w1_raw[u][:, :, PACK * ms.start : PACK * ms.stop].rearrange("p j (m t) -> " + walk, t=PACK),
            )
        w1_codes = sb([P, H], U32, "w1_codes")
        w1_scale = sb([P, H], U8, "w1_scale")
        for first, last in ((0, 1), (1, 2), (2, PACK)):
            cols = slice(P * first, P * last)
            quantise(w1_codes[:, cols], w1_scale[:, cols], w1_bf[:, first:last].rearrange("p t m j -> p (t m j)"))

        y = [sb([P, S], F32, "y%d" % t) for t in range(PACK)]
        pieces = [(0, first, BANK // 2) for first in range(0, S, BANK // 2)]
        pieces = pieces + [(t, first, BANK) for t in range(1, PACK) for first in range(0, S, BANK)]
        for number, (t, first, width) in enumerate(pieces):
            cols, dealt = slice(first, first + width), slice(P * t, P * (t + 1))
            acc = bank(number % BANKS, [P, width])
            multiply(acc[:], w1_codes[:, dealt].bitcast(FP8X4), w1_scale[:, dealt], xg[:, cols], sg[:, cols])
            copy = nc.vector.tensor_copy if t == 0 and number % 2 == 1 else nc.scalar.copy
            copy(out=y[t][:, cols], in_=acc[:])

        w2_bf = sb([P, PACK, P, PACK], BF16, "w2_bf")
        w2_scale = sb([P, H], U8, "w2_scale")
        for piece in range(W2_PIECES):
            copy, walk = (nc.scalar.copy, "p m j t") if piece == W2_PIECES - 1 else (nc.gpsimd.tensor_copy, "p t m j")
            copy(
                out=w2_bf[:, :, 32 * piece : 32 * (piece + 1), :].rearrange("p t m j -> " + walk),
                in_=w2_raw[:, :, P * piece : P * (piece + 1)].rearrange("p j (m t) -> " + walk, t=PACK),
            )

        def add_turned(sums, t, terms, opens, closes):
            steps = [(b, term) for b in range(2) for term in terms]
            for i, (b, term) in enumerate(steps):
                nc.tensor.matmul(
                    out=sums[:, b, t % 2, :],
                    lhsT=term[:, P * b : P * (b + 1)],
                    rhs=ident[:],
                    is_transpose=True,
                    start=(opens and i == 0),
                    stop=(closes and i == len(steps) - 1),
                )

        def gather(half, t, ln, sums):
            entries = n1_t[:, half * 2 * VH // LIST_ROWS : (half + 1) * 2 * VH // LIST_ROWS]
            nc.vector.tensor_copy(out=ln.rearrange("p v e -> p (v e)"), in_=y[t][:].indirect(entries))
            add_turned(sums, t, (ln[:, :, 0], ln[:, :, 1]), t % 2 == 0, False)

        def distance(first, ln, diff, dist, sums, engine):
            engine.tensor_tensor(out=diff, in0=ln[:, :, :, 0], in1=ln[:, :, :, 1], op=ALU.subtract)
            nc.scalar.activation(out=dist, in_=diff, func=ACT.Abs, scale=3.0)
            for e in range(ln.shape[1]):
                add_turned(sums, first + e, (dist[:, e],), False, (first + e) % 2 == 1)

        def turn_back(half, u, sums, back, tag=None):
            zt = sb([P, 2, P, 2], BF16, "zt%d_%d" % (half, u), tag=tag)
            nc.scalar.activation(out=zt[:], in_=sums[:].rearrange("v b e p -> v b p e"), func=ACT.Copy, scale=0.25)
            words = zt[:].rearrange("v b p e -> v (b p e)").bitcast(F32)
            for b in range(2):
                nc.tensor.transpose(back[:, b, u, :], words[:, P * b : P * (b + 1)], ident[:])

        def interleave(half, back):
            z_words = sb([P, 2, P, 2], F32, "z_words%d" % half)
            nc.scalar.copy(out=z_words[:], in_=back[:].rearrange("p b u v -> p b v u"))
            return z_words

        def second_layer(half, z_words, banks):
            z_codes = sb([P, VH], U32, "z_codes%d" % half)
            z_scale = sb([P, VH], U8, "z_scale%d" % half)
            quantise(z_codes[:], z_scale[:], z_words[:].rearrange("p b v u -> p (b v u)").bitcast(BF16))
            accs = {}
            for u in banks:
                accs[u] = bank(banks[u], [P, 2, VH])
                for e in range(2):
                    dealt = slice(P * (2 * u + e), P * (2 * u + e + 1))
                    multiply(accs[u][:, e, :], w2_codes[:, dealt].bitcast(FP8X4), w2_scale[:, dealt], z_codes[:], z_scale[:])
            return accs

        def work_tiles(name, planes, ln_tag=None, dist_tag=None):
            ln = sb([P, planes, VH, 2], F32, "ln" + name, tag=ln_tag)
            diff = sb([P, planes, VH], F32, "diff" + name)
            dist = sb([P, planes, VH], F32, "dist" + name, tag=dist_tag)
            return ln, diff, dist

        sums_lo, sums_hi, back_a = bank(2, [P, 2, 2, P]), bank(3, [P, 2, 2, P]), bank(1, [P, 2, 2, P])
        ln_a01, diff_a01, dist_a01 = work_tiles("A01", 2)
        for t in range(2):
            gather(0, t, ln_a01[:, t], sums_lo)
        distance(0, ln_a01[:], diff_a01[:], dist_a01[:], sums_lo, nc.gpsimd)
        tiles_a = {t: work_tiles("A%d" % t, 1) for t in (2, 3)}
        for t in (2, 3):
            gather(0, t, tiles_a[t][0][:, 0], sums_hi)
        for t in (2, 3):
            distance(t, tiles_a[t][0][:], tiles_a[t][1][:], tiles_a[t][2][:], sums_hi, nc.gpsimd)
        turn_back(0, 0, sums_lo, back_a, "diffA3")
        turn_back(0, 1, sums_hi, back_a)
        z_words_a = interleave(0, back_a)

        sums_lo, sums_hi, back_b = bank(3, [P, 2, 2, P]), bank(1, [P, 2, 2, P]), bank(0, [P, 2, 2, P])
        ln_b, diff_b, dist_b = work_tiles("B012", 3, "diffA01", "zt0_1")
        for t in range(3):
            gather(1, t, ln_b[:, t], sums_lo if t < 2 else sums_hi)
        w2_codes = sb([P, H], U32, "w2_codes", tag="y2")
        quantise(w2_codes[:], w2_scale[:], w2_bf[:].rearrange("p t m j -> p (t m j)"))
        accs_a = second_layer(0, z_words_a, {0: 4, 1: 5})
        h01 = [sb([P, 2, VH], F32, "h01_%d" % half) for half in range(2)]
        nc.scalar.copy(out=h01[0][:], in_=accs_a[0][:])
        distance(0, ln_b[:, 0:2], diff_b[:, 0:2], dist_b[:, 0:2], sums_lo, nc.gpsimd)
        late = sb([P, 3, VH], F32, "late", tag="z_words0")
        ln_b3 = late[:, 0:2].rearrange("p a (b e) -> p (a b) e", e=2)
        gather(1, 3, ln_b3, sums_hi)
        distance(2, ln_b[:, 2:3], late[:, 2:3], dist_b[:, 2:3], sums_hi, nc.gpsimd)
        turn_back(1, 0, sums_lo, back_b)
        h2_a = sb([P, VH], F32, "h2_a")
        nc.scalar.copy(out=h2_a[:], in_=accs_a[1][:, 0])
        dist_b3 = sb([P, 1, VH], F32, "dist_b3")
        distance(3, ln_b3.unsqueeze(1), diff_b[:, 2:3], dist_b3[:], sums_hi, nc.vector)

        w3w = sb([P, PACK, P, 2], U8, "w3w", tag="z_words0")
        w3s = sb([P, PACK, P], U8, "w3s", tag="diffB012")
        nc.gpsimd.tensor_copy(out=w3w[:], in_=w3w_raw[:].rearrange("p (m t b) -> p t m b", t=PACK, b=2))
        nc.gpsimd.tensor_copy(out=w3s[:], in_=w3s_raw[:].rearrange("p (m t) -> p t m", t=PACK))
        turn_back(1, 1, sums_hi, back_b)
        z_words_b = interleave(1, back_b)
        h3_a = sb([P, VH], F32, "h3_a", tag="zt1_1")
        nc.scalar.copy(out=h3_a[:], in_=accs_a[1][:, 1])

        def scatter(half, t, values):
            entries = n2_t[:, half * VH // LIST_ROWS : (half + 1) * VH // LIST_ROWS]
            nc.vector.tensor_copy(out=page[t][:].indirect(entries), in_=values)

        starts = [sum(CHUNKS[:i]) for i in range(len(CHUNKS))]
        pairs = [sb([P, 2, width, 2], BF16, "pairs%d" % i) for i, width in enumerate(CHUNKS)]

        def round_page(t, i):
            copy = nc.gpsimd.tensor_copy if t < 2 and i >= SCALAR_CHUNKS else nc.scalar.copy
            copy(out=pairs[i][:, t // 2, :, t % 2], in_=page[t][:, starts[i] : starts[i] + CHUNKS[i]])

        scatter(0, 0, h01[0][:, 0, :])
        scatter(0, 1, h01[0][:, 1, :])
        scatter(0, 2, h2_a[:])
        accs_b = second_layer(1, z_words_b, {1: 7, 0: 6})
        h2_b = sb([P, VH], F32, "h2_b")
        h3_b = sb([P, VH], F32, "h3_b", tag="z_codes1")
        nc.scalar.copy(out=h2_b[:], in_=accs_b[1][:, 0])
        nc.scalar.copy(out=h01[1][:], in_=accs_b[0][:])
        nc.scalar.copy(out=h3_b[:], in_=accs_b[1][:, 1])
        scatter(0, 3, h3_a[:])
        scatter(1, 2, h2_b[:])
        scatter(1, 0, h01[1][:, 0, :])
        scatter(1, 1, h01[1][:, 1, :])
        scatter(1, 3, h3_b[:])
        for t in (2, 0, 1):
            for i in range(len(CHUNKS)):
                round_page(t, i)

        out_rows = out_0.rearrange("(p t) w -> p t w", t=PACK)
        out_words = out_1[0].rearrange("p n t -> p (n t)").bitcast(I32)
        o_scale = sb([P, U], U8, "o_scale")
        z2_mx, o32 = {}, {}

        def quantise_page(i):
            round_page(PACK - 1, i)
            z2_words = sb([P, CHUNKS[i], 2], F32, "z2_words%d" % i)
            join = nc.vector.tensor_copy if i < VECTOR_JOINS else nc.scalar.copy
            join(out=z2_words[:], in_=pairs[i][:].rearrange("p u w e -> p u (w e)").bitcast(F32).rearrange("p u w -> p w u"))
            z2_mx[i] = (sb([P, CHUNKS[i]], U32, "z2_codes%d" % i), sb([P, CHUNKS[i]], U8, "z2_scale%d" % i))
            quantise(z2_mx[i][0][:], z2_mx[i][1][:], z2_words[:].rearrange("p w u -> p (w u)").bitcast(BF16))

        def last_layer(i):
            cols = slice(starts[i], starts[i] + CHUNKS[i])
            o32[i] = sb([P, PACK, CHUNKS[i]], F32, "o32_%d" % i)
            per_bank = BANK // CHUNKS[i]
            for b in range(PACK // per_bank):
                acc = bank(starts[i] // P + b, [P, per_bank, CHUNKS[i]])
                for e in range(per_bank):
                    t = per_bank * b + e
                    weights = w3w[:, t].rearrange("p m b -> p (m b)").bitcast(FP4X4)
                    multiply(acc[:, e, :], weights, w3s[:, t, :], z2_mx[i][0][:], z2_mx[i][1][:])
                planes = slice(per_bank * b, per_bank * (b + 1))
                nc.vector.tensor_tensor(out=o32[i][:, planes, :], in0=acc[:], in1=res_t[:, planes, cols], op=ALU.add)
                nc.sync.dma_start(out=out_rows[:, planes, cols], in_=o32[i][:, planes, :])

        o_codes = sb([P, U], I32, "o_codes")

        def hand_on(i):
            cols = slice(starts[i], starts[i] + CHUNKS[i])
            o_bf = sb([P, CHUNKS[i], PACK], BF16, "o_bf%d" % i)
            weave = nc.vector.tensor_copy if i == len(CHUNKS) - 1 else nc.scalar.copy
            weave(out=o_bf[:].rearrange("p (c n) t -> p c t n", n=4), in_=o32[i][:].rearrange("p t (c n) -> p c t n", n=4))
            quantise(o_codes[:, cols], o_scale[:, cols], o_bf[:].rearrange("p w t -> p (w t)"))
            if cols.stop in CODE_STORES:
                stored = slice(CODE_STORES[CODE_STORES.index(cols.stop) - 1], cols.stop)
                nc.sync.dma_start(out=out_words[:, stored], in_=o_codes[:, stored])

        quantise_page(0)
        quantise_page(1)
        for i in range(len(CHUNKS)):
            last_layer(i)
            if i + 2 < len(CHUNKS):
                quantise_page(i + 2)
            hand_on(i)
        for q in range(4):
            queue = nc.scalar if q < 3 else nc.sync
            queue.dma_start(out=out_2[0, 4 * q : 4 * q + 4, :].bitcast(I32), in_=o_scale[32 * q : 32 * q + 4, :].bitcast(I32))
